import numpy as np
import ml_dtypes


def mxq(x, axis, fmt="e4m3"):
    dtype, down = {"e4m3": (ml_dtypes.float8_e4m3fn, 7), "e5m2": (ml_dtypes.float8_e5m2, 14)}[fmt]
    v = np.moveaxis(np.asarray(x, np.float32).astype(ml_dtypes.bfloat16).astype(np.float64), axis, -1)
    blocks = v.reshape(v.shape[:-1] + (-1, 32))
    amax = np.abs(blocks).max(-1, keepdims=True)
    byte = np.maximum(np.where(amax > 0, np.frexp(amax)[1] - 1 + 127, 0) - down, 1)
    scale = np.exp2(byte - 127.0)
    codes = (blocks / scale).astype(np.float32).astype(dtype).astype(np.float64)
    return np.moveaxis((codes * scale).reshape(v.shape), -1, axis)


WIDE = False


def mx_kscale(k):
    if not WIDE:
        return np.ones(k)
    levels = np.array([10, -10, 5, -5, 0])
    if k % 512:
        return np.exp2(np.random.permutation(np.resize(levels, k // 32))).repeat(32)
    a = np.empty((k // 512, 16))
    for p in range(k // 512):
        a[p, :8] = np.random.permutation(np.resize(levels, 8))
        for g in range(8):
            far = levels[np.abs(levels - a[p, g]) >= 10]
            a[p, g + 8] = far[np.random.randint(len(far))]
    return np.exp2(a.ravel()).repeat(32)


def f64(x):
    return np.asarray(x).astype(np.float64)


def striped(idx):
    return np.tile(idx.reshape(-1, 16).T, (8, 1)).astype(np.uint16)


def unstriped(offs):
    return offs[:16].T.reshape(-1).astype(np.int64)


def striped8(idx):
    return np.concatenate([x.reshape(-1, 16).T for x in idx]).astype(np.uint16)


def runs(offs, k):
    lists = np.stack([offs[16 * r : 16 * r + 16].T.reshape(-1) for r in range(8)]).astype(np.int64)
    return lists[np.arange(k) % 512 // 64]


def pack_weight(w):
    k, n = w.shape
    w = f64(np.asarray(w, np.float32).astype(ml_dtypes.bfloat16)).reshape(k // 32, 32, n)
    amax = np.abs(w).max(1)
    byte = np.clip(np.where(amax > 0, np.frexp(amax)[1] - 1 + 127 - 7, 1), 1, 254)
    scaled = (w * np.exp2(127.0 - byte)[:, None, :]).reshape(k, n).astype(np.float32)
    words = np.ascontiguousarray(scaled.reshape(k // 512, 128, 4, n).transpose(0, 1, 3, 2)).astype(ml_dtypes.float8_e4m3fn).view(np.uint8)
    return words, np.ascontiguousarray(byte.astype(np.uint8).reshape(k // 512, 16, n))


def unpack_weight(words, scales):
    g, p, n, _ = words.shape
    vals = np.ascontiguousarray(words).view(ml_dtypes.float8_e4m3fn).astype(np.float64) * np.repeat(np.exp2(scales.astype(np.float64) - 127.0), 8, axis=1)[..., None]
    return vals.transpose(0, 1, 3, 2).reshape(g * 512, n)


def sigmoid(v):
    return 1.0 / (1.0 + np.exp(-np.maximum(v, -700.0)))


K, T, S, H, C = 512, 2048, 512, 512, 512


def setup_inputs():
    n = np.random.standard_normal
    s = mx_kscale(K)[:, None]
    packed_xT = pack_weight(n((K, T)) * s)
    return {
        "x_words": packed_xT[0],
        "x_scales": packed_xT[1],
        "w1": (n((K, H)) / np.sqrt(K) / s).astype(np.float32),
        "w2": (n((K, H)) / np.sqrt(K) / s).astype(np.float32),
        "gs": (np.random.uniform(0.5, 1.5, (K, 1)) / s).astype(np.float32),
        "offs": striped(np.random.permutation(T)[:S]),
        "two": striped(np.random.permutation(T)[:S]),
        "n1": striped8(np.stack([np.random.permutation(S) for _ in range(8)])),
        "n2": striped8(np.stack([np.random.permutation(S) for _ in range(8)])),
        "n3": striped8(np.stack([np.random.permutation(S) for _ in range(8)])),
        "cand": striped(np.random.permutation(T)[:C]),
        "n4": striped8(np.stack([np.random.permutation(S) for _ in range(8)])),
        "n5": striped8(np.stack([np.random.permutation(S) for _ in range(8)])),
    }


def reference(x_words, x_scales, w1, w2, gs, offs, two, n1, n2, n3, cand, n4, n5):
    x_cand = unpack_weight(x_words, x_scales)[:, unstriped(cand)]
    xq = unpack_weight(x_words, x_scales)[:, unstriped(offs)]
    y = mxq(f64(w1), 0, "e4m3").T @ xq
    x_two = unpack_weight(x_words, x_scales)[:, unstriped(two)]
    d = mxq(f64(w2), 0, "e4m3").T @ x_two
    z = f64(gs) * (np.maximum(np.minimum(y - (0.5 * (y[np.arange(H)[:, None], runs(n1, H)])), d[np.arange(H)[:, None], runs(n2, H)]), d[np.arange(H)[:, None], runs(n3, H)]))
    s = 0.0625 * ((x_cand.T @ mxq(z, 0, "e4m3")))
    st = s * (sigmoid(s[np.arange(C)[:, None], runs(n4, C)]))
    return st - (st[np.arange(C)[:, None], runs(n5, C)])

@@ -1,0 +1,234 @@
+from contextlib import ExitStack
+
+import concourse.mybir as mybir
+
+K, T, S = 512, 2048, 512
+P = 128
+PACK = 4
+HALF = 256
+FLOPS = 3 * 2 * 512 * 512 * 512
+
+F32 = mybir.dt.float32
+BF16 = mybir.dt.bfloat16
+I32 = mybir.dt.int32
+U32 = mybir.dt.uint32
+U16 = mybir.dt.uint16
+U8 = mybir.dt.uint8
+FP8X4 = mybir.dt.float8_e4m3fn_x4
+ALU = mybir.AluOpType
+ACT = mybir.ActivationFunctionType
+
+
+def tile_picked_twcclampbhopg_none_p_kernel(
+    tc, x_words, x_scales, w1, w2, gs, offs, two, n1, n2, n3, cand, n4, n5, out
+):
+    nc = tc.nc
+    with ExitStack() as ctx:
+        lists = ctx.enter_context(tc.tile_pool(name="lists", bufs=1))
+        keep = ctx.enter_context(tc.tile_pool(name="keep", bufs=1))
+        psum = ctx.enter_context(tc.psum_pool(name="psum", bufs=1))
+
+        def load_list(name, src):
+            tile = lists.tile([P, S // 16], U16, name=name)
+            nc.sync.dma_start(tile[:], src)
+            return tile
+
+        def load_half(name, w, h):
+            rows = w.rearrange("(p j) c -> p j c", j=PACK)
+            raw = keep.tile([P, PACK, HALF], F32, name="%s_raw%d" % (name, h))
+            nc.sync.dma_start(raw[:], rows[:, :, h * HALF : (h + 1) * HALF])
+            return raw
+
+        def part(lst, h):
+            return lst[:, h * (HALF // 16) : (h + 1) * (HALF // 16)]
+
+        def cols(h):
+            return slice(h * HALF, (h + 1) * HALF)
+
+        warm = keep.tile([P, 2], F32, name="warm")
+        nc.vector.memset(warm[:, 0:1], 0.0)
+        xs = keep.tile([P, T], U8, name="xs", align_bytes=64)
+        nc.vector.memset(xs[:].bitcast(I32), 0)
+        nc.scalar.activation(warm[:, 1:2], warm[:, 0:1], ACT.Sigmoid)
+        scale_rows = x_scales[0].bitcast(I32)
+
+        w2_raw = [load_half("w2", w2, 0)]
+        for r in range(4):
+            nc.sync.dma_start(xs[r:P:32, :].bitcast(I32), scale_rows[r:16:4, :])
+        two_l = load_list("two_l", two)
+        offs_l = load_list("offs_l", offs)
+        w2_raw.append(load_half("w2", w2, 1))
+        xw = keep.tile([P, T], U32, name="xw", align_bytes=64)
+        nc.sync.dma_start(xw[:].bitcast(I32), x_words[0].rearrange("p n t -> p (n t)").bitcast(I32))
+        cand_l = load_list("cand_l", cand)
+        g_t = keep.tile([P, PACK], F32, name="g_t")
+        nc.sync.dma_start(g_t[:], gs.rearrange("(p t) o -> p (t o)", t=PACK))
+        n2_l = load_list("n2_l", n2)
+        n3_l = load_list("n3_l", n3)
+        w1_raw = [load_half("w1", w1, h) for h in range(2)]
+        n1_l = load_list("n1_l", n1)
+        n4_l = load_list("n4_l", n4)
+        n5_l = load_list("n5_l", n5)
+
+        def cast_weight(name, parts):
+            grouped = keep.tile([P, PACK * K], BF16, name=name + "_bf", align_bytes=64)
+            view = grouped[:].rearrange("p (t m j) -> p m j t", t=PACK, j=PACK)
+            for h in range(2):
+                nc.scalar.copy(
+                    view[:, h * 64 : (h + 1) * 64],
+                    parts[h][:].rearrange("p j (m t) -> p m j t", t=PACK),
+                )
+            return grouped
+
+        def quantize_weight(name, grouped, widths):
+            codes = keep.tile([P, K], U32, name=name + "_codes", align_bytes=64)
+            scales = keep.tile([P, K], U8, name=name + "_scales", align_bytes=64)
+            c0 = 0
+            for width in widths:
+                nc.vector.quantize_mx(
+                    out=codes[:, c0 : c0 + width].bitcast(FP8X4),
+                    scales=scales[:, c0 : c0 + width],
+                    in_=grouped[:, PACK * c0 : PACK * (c0 + width)],
+                )
+                c0 = c0 + width
+            return codes, scales
+
+        def pick_bytes(name, lst):
+            picked = keep.tile([P, S], U8, name=name, align_bytes=64)
+            nc.vector.tensor_copy(picked[:], xs[:].indirect(lst[:]))
+            return picked
+
+        def pick_words(name, lst):
+            picked = keep.tile([P, S], U32, name=name, align_bytes=64)
+            nc.vector.tensor_copy(picked[:], xw[:].indirect(lst[:]))
+            return picked
+
+        w2_bf = cast_weight("w2", w2_raw)
+        two_b = pick_bytes("two_b", two_l)
+        offs_b = pick_bytes("offs_b", offs_l)
+        cand_b0 = pick_bytes("cand_b0", cand_l)
+        w2_c, w2_s = quantize_weight("w2", w2_bf, [128, 128, 256])
+        two_w = pick_words("two_w", two_l)
+
+        mag = keep.tile([P, PACK], F32, name="mag")
+        sgn = keep.tile([P, PACK], F32, name="sgn")
+        neg = keep.tile([P, PACK], F32, name="neg")
+        nc.scalar.activation(mag[:], g_t[:], ACT.Abs)
+        nc.scalar.activation(sgn[:], g_t[:], ACT.Sign)
+        nc.scalar.activation(neg[:], mag[:], ACT.Copy, scale=-0.5)
+
+        def product(bank, codes, scales, t, words, sbytes, c):
+            m = slice(t * P, (t + 1) * P)
+            nc.tensor.matmul_mx(
+                out=bank[:, c],
+                lhsT=codes[:, m].bitcast(FP8X4),
+                lhsT_scale=scales[:, m],
+                rhs=words[:, c].bitcast(FP8X4),
+                rhs_scale=sbytes[:, c],
+                start=True,
+                stop=True,
+            )
+
+        every = slice(0, S)
+        offs_w = pick_words("offs_w", offs_l)
+        d_t = []
+        for t in range(PACK):
+            bank = psum.tile([P, S], F32, name="bank_d%d" % t, tag="a%d" % t)
+            product(bank, w2_c, w2_s, t, two_w, two_b, every)
+            d = keep.tile([P, S], F32, name="d%d" % t)
+            nc.scalar.activation(d[:], bank[:], ACT.Copy, scale=mag[:, t : t + 1])
+            d_t.append(d)
+
+        w1_bf = cast_weight("w1", w1_raw)
+        cand_b = keep.tile([P, S], U8, name="cand_b", align_bytes=64)
+        nc.vector.tensor_copy(
+            cand_b[:].rearrange("p (t m) -> p t m", t=PACK),
+            cand_b0[:].rearrange("p (m t) -> p t m", t=PACK),
+        )
+
+        b_t = [keep.tile([P, S], BF16, name="b%d" % t) for t in range(PACK)]
+        c_t = [keep.tile([P, S], BF16, name="c%d" % t) for t in range(PACK)]
+
+        def fetch_d(t, h):
+            nc.vector.tensor_copy(b_t[t][:, cols(h)], d_t[t][:].indirect(part(n2_l, h)))
+            nc.vector.tensor_copy(c_t[t][:, cols(h)], d_t[t][:].indirect(part(n3_l, h)))
+
+        for t in range(PACK):
+            fetch_d(t, 0)
+        w1_c, w1_s = quantize_weight("w1", w1_bf, [512])
+        y_t, yh_t = [], []
+        for t in range(PACK):
+            bank = psum.tile([P, S], F32, name="bank_y%d" % t, tag="b%d" % t)
+            product(bank, w1_c, w1_s, t, offs_w, offs_b, every)
+            y = keep.tile([P, S], F32, name="y%d" % t)
+            yh = keep.tile([P, S], F32, name="yh%d" % t)
+            nc.scalar.activation(yh[:], bank[:], ACT.Copy, scale=neg[:, t : t + 1])
+            nc.scalar.activation(y[:], bank[:], ACT.Copy, scale=mag[:, t : t + 1])
+            y_t.append(y)
+            yh_t.append(yh)
+
+        cand_w = keep.tile([P, S], U32, name="cand_w", align_bytes=64)
+        nc.vector.tensor_copy(
+            cand_w[:].rearrange("p (t m) -> p m t", t=PACK), xw[:].indirect(cand_l[:])
+        )
+        for t in range(PACK):
+            fetch_d(t, 1)
+
+        z_c = keep.tile([P, S], U32, name="z_c", align_bytes=64)
+        z_s = keep.tile([P, S], U8, name="z_s", align_bytes=64)
+        s_bank = [psum.tile([P, S], F32, name="bank_s%d" % t, tag="a%d" % t) for t in range(PACK)]
+        s_t = [keep.tile([P, S], F32, name="s%d" % t) for t in range(PACK)]
+        for h in range(2):
+            z_bf = keep.tile([P, HALF, PACK], BF16, name="z_bf%d" % h, align_bytes=64)
+            a_t = [keep.tile([P, HALF], F32, name="a%d_%d" % (t, h)) for t in range(PACK)]
+            lo_t = [keep.tile([P, HALF], BF16, name="lo%d_%d" % (t, h)) for t in range(PACK)]
+            hi_t = [keep.tile([P, HALF], BF16, name="hi%d_%d" % (t, h)) for t in range(PACK)]
+            for step in range(PACK + 2):
+                if step < PACK:
+                    t = step
+                    nc.vector.tensor_tensor(
+                        a_t[t][:], yh_t[t][:].indirect(part(n1_l, h)), y_t[t][:, cols(h)], ALU.add
+                    )
+                if 1 <= step <= PACK:
+                    t = step - 1
+                    nc.vector.tensor_tensor(lo_t[t][:], a_t[t][:], b_t[t][:, cols(h)], ALU.min)
+                if step >= 2:
+                    t = step - 2
+                    nc.vector.tensor_tensor(hi_t[t][:], lo_t[t][:], c_t[t][:, cols(h)], ALU.max)
+                    nc.scalar.activation(z_bf[:, :, t], hi_t[t][:], ACT.Copy, scale=sgn[:, t : t + 1])
+            nc.vector.quantize_mx(
+                out=z_c[:, cols(h)].bitcast(FP8X4),
+                scales=z_s[:, cols(h)],
+                in_=z_bf[:].rearrange("p c t -> p (c t)"),
+            )
+            for t in range(PACK):
+                product(s_bank[t], cand_w, cand_b, t, z_c, z_s, cols(h))
+                if h == 0 or t == 0:
+                    nc.scalar.activation(s_t[t][:, cols(h)], s_bank[t][:, cols(h)], ACT.Copy, scale=0.0625)
+                else:
+                    nc.vector.tensor_scalar_mul(s_t[t][:, cols(h)], s_bank[t][:, cols(h)], 0.0625)
+
+        out_rows = out.rearrange("(p t) j -> t p j", t=PACK)
+        sig_t = [keep.tile([P, S], F32, name="sig%d" % t) for t in range(PACK)]
+        st_t = [keep.tile([P, S], F32, name="st%d" % t) for t in range(PACK)]
+        for t in range(PACK):
+            for h in range(2):
+                nc.scalar.activation(sig_t[t][:, cols(h)], s_t[t][:].indirect(part(n4_l, h)), ACT.Sigmoid)
+            nc.vector.tensor_tensor(st_t[t][:], s_t[t][:], sig_t[t][:], ALU.mult)
+        for t in range(PACK):
+            if t in [0]:
+                for h in range(2):
+                    far = keep.tile([P, HALF], F32, name="far%d_%d" % (t, h))
+                    nc.vector.tensor_copy(far[:], st_t[t][:].indirect(part(n5_l, h)))
+                    res = keep.tile([P, HALF], F32, name="res%d_%d" % (t, h))
+                    nc.vector.tensor_tensor(res[:], st_t[t][:, cols(h)], far[:], ALU.subtract)
+                    nc.sync.dma_start(out_rows[t][:, cols(h)], res[:])
+            else:
+                minus = keep.tile([P, S], F32, name="minus%d" % t)
+                nc.scalar.activation(minus[:], st_t[t][:], ACT.Copy, scale=-1.0)
+                for h in range(2):
+                    res = keep.tile([P, HALF], F32, name="res%d_%d" % (t, h))
+                    nc.vector.tensor_tensor(
+                        res[:], minus[:].indirect(part(n5_l, h)), st_t[t][:, cols(h)], ALU.add
+                    )
+                    nc.sync.dma_start(out_rows[t][:, cols(h)], res[:])

@@ -6,6 +6,7 @@ K, T, S = 512, 2048, 512
 P = 128
 PACK = 4
 HALF = 256
+FIRST = 256
 FLOPS = 3 * 2 * 512 * 512 * 512
 
 F32 = mybir.dt.float32
@@ -28,36 +29,38 @@ def tile_picked_twcclampbhopg_none_p_kernel(
         keep = ctx.enter_context(tc.tile_pool(name="keep", bufs=1))
         psum = ctx.enter_context(tc.psum_pool(name="psum", bufs=1))
 
+        every = slice(0, S)
+        halves = [slice(0, HALF), slice(HALF, S)]
+
         def load_list(name, src):
             tile = lists.tile([P, S // 16], U16, name=name)
             nc.sync.dma_start(tile[:], src)
             return tile
 
-        def load_half(name, w, h):
-            rows = w.rearrange("(p j) c -> p j c", j=PACK)
-            raw = keep.tile([P, PACK, HALF], F32, name="%s_raw%d" % (name, h))
-            nc.sync.dma_start(raw[:], rows[:, :, h * HALF : (h + 1) * HALF])
-            return raw
+        def load_columns(name, w, c):
+            raw = keep.tile([P, PACK, c.stop - c.start], F32, name="%s_raw%d" % (name, c.start))
+            nc.sync.dma_start(raw[:], w.rearrange("(p j) c -> p j c", j=PACK)[:, :, c])
+            return c, raw
 
-        def part(lst, h):
-            return lst[:, h * (HALF // 16) : (h + 1) * (HALF // 16)]
-
-        def cols(h):
-            return slice(h * HALF, (h + 1) * HALF)
+        def entries(lst, c):
+            return lst[:, c.start // 16 : c.stop // 16]
 
         warm = keep.tile([P, 2], F32, name="warm")
-        nc.vector.memset(warm[:, 0:1], 0.0)
         xs = keep.tile([P, T], U8, name="xs", align_bytes=64)
         nc.vector.memset(xs[:].bitcast(I32), 0)
+        nc.vector.memset(warm[:, 0:1], 0.0)
         nc.scalar.activation(warm[:, 1:2], warm[:, 0:1], ACT.Sigmoid)
-        scale_rows = x_scales[0].bitcast(I32)
+        wide = [keep.tile([P, 2 * S], F32, name="wide%d" % t) for t in range(PACK)]
+        for t in range(PACK):
+            nc.vector.memset(wide[t][:, S:], 0.0)
 
-        w2_raw = [load_half("w2", w2, 0)]
+        w2_raw = [load_columns("w2", w2, slice(0, FIRST))]
+        scale_rows = x_scales[0].bitcast(I32)
         for r in range(4):
             nc.sync.dma_start(xs[r:P:32, :].bitcast(I32), scale_rows[r:16:4, :])
         two_l = load_list("two_l", two)
         offs_l = load_list("offs_l", offs)
-        w2_raw.append(load_half("w2", w2, 1))
+        w2_raw.append(load_columns("w2", w2, slice(FIRST, K)))
         xw = keep.tile([P, T], U32, name="xw", align_bytes=64)
         nc.sync.dma_start(xw[:].bitcast(I32), x_words[0].rearrange("p n t -> p (n t)").bitcast(I32))
         cand_l = load_list("cand_l", cand)
@@ -65,18 +68,18 @@ def tile_picked_twcclampbhopg_none_p_kernel(
         nc.sync.dma_start(g_t[:], gs.rearrange("(p t) o -> p (t o)", t=PACK))
         n2_l = load_list("n2_l", n2)
         n3_l = load_list("n3_l", n3)
-        w1_raw = [load_half("w1", w1, h) for h in range(2)]
+        w1_raw = [load_columns("w1", w1, c) for c in halves]
         n1_l = load_list("n1_l", n1)
         n4_l = load_list("n4_l", n4)
         n5_l = load_list("n5_l", n5)
 
         def cast_weight(name, parts):
-            grouped = keep.tile([P, PACK * K], BF16, name=name + "_bf", align_bytes=64)
+            grouped = keep.tile([P, PACK * K], BF16, name=name + "_bf", align_bytes=64, tag=name + "_bf")
             view = grouped[:].rearrange("p (t m j) -> p m j t", t=PACK, j=PACK)
-            for h in range(2):
+            for c, raw in parts:
                 nc.scalar.copy(
-                    view[:, h * 64 : (h + 1) * 64],
-                    parts[h][:].rearrange("p j (m t) -> p m j t", t=PACK),
+                    view[:, c.start // PACK : c.stop // PACK],
+                    raw[:].rearrange("p j (m t) -> p m j t", t=PACK),
                 )
             return grouped
 
@@ -103,6 +106,18 @@ def tile_picked_twcclampbhopg_none_p_kernel(
             nc.vector.tensor_copy(picked[:], xw[:].indirect(lst[:]))
             return picked
 
+        def product(result, codes, scales, t, words, sbytes, c):
+            m = slice(t * P, (t + 1) * P)
+            nc.tensor.matmul_mx(
+                out=result,
+                lhsT=codes[:, m].bitcast(FP8X4),
+                lhsT_scale=scales[:, m],
+                rhs=words[:, c].bitcast(FP8X4),
+                rhs_scale=sbytes[:, c],
+                start=True,
+                stop=True,
+            )
+
         w2_bf = cast_weight("w2", w2_raw)
         two_b = pick_bytes("two_b", two_l)
         offs_b = pick_bytes("offs_b", offs_l)
@@ -114,52 +129,38 @@ def tile_picked_twcclampbhopg_none_p_kernel(
         sgn = keep.tile([P, PACK], F32, name="sgn")
         neg = keep.tile([P, PACK], F32, name="neg")
         nc.scalar.activation(mag[:], g_t[:], ACT.Abs)
-        nc.scalar.activation(sgn[:], g_t[:], ACT.Sign)
         nc.scalar.activation(neg[:], mag[:], ACT.Copy, scale=-0.5)
+        nc.scalar.activation(sgn[:], g_t[:], ACT.Sign)
 
-        def product(bank, codes, scales, t, words, sbytes, c):
-            m = slice(t * P, (t + 1) * P)
-            nc.tensor.matmul_mx(
-                out=bank[:, c],
-                lhsT=codes[:, m].bitcast(FP8X4),
-                lhsT_scale=scales[:, m],
-                rhs=words[:, c].bitcast(FP8X4),
-                rhs_scale=sbytes[:, c],
-                start=True,
-                stop=True,
-            )
-
-        every = slice(0, S)
         offs_w = pick_words("offs_w", offs_l)
-        d_t = []
         for t in range(PACK):
             bank = psum.tile([P, S], F32, name="bank_d%d" % t, tag="a%d" % t)
-            product(bank, w2_c, w2_s, t, two_w, two_b, every)
-            d = keep.tile([P, S], F32, name="d%d" % t)
-            nc.scalar.activation(d[:], bank[:], ACT.Copy, scale=mag[:, t : t + 1])
-            d_t.append(d)
+            product(bank[:], w2_c, w2_s, t, two_w, two_b, every)
+            nc.scalar.activation(wide[t][:, every], bank[:], ACT.Copy, scale=mag[:, t : t + 1])
 
-        w1_bf = cast_weight("w1", w1_raw)
         cand_b = keep.tile([P, S], U8, name="cand_b", align_bytes=64)
         nc.vector.tensor_copy(
-            cand_b[:].rearrange("p (t m) -> p t m", t=PACK),
-            cand_b0[:].rearrange("p (m t) -> p t m", t=PACK),
+            cand_b[:].bitcast(I32).rearrange("p (t g r) -> p t g r", t=PACK, g=8),
+            cand_b0[:].bitcast(I32).rearrange("p (g t r) -> p t g r", t=PACK, g=8),
         )
-
-        b_t = [keep.tile([P, S], BF16, name="b%d" % t) for t in range(PACK)]
-        c_t = [keep.tile([P, S], BF16, name="c%d" % t) for t in range(PACK)]
-
-        def fetch_d(t, h):
-            nc.vector.tensor_copy(b_t[t][:, cols(h)], d_t[t][:].indirect(part(n2_l, h)))
-            nc.vector.tensor_copy(c_t[t][:, cols(h)], d_t[t][:].indirect(part(n3_l, h)))
-
-        for t in range(PACK):
-            fetch_d(t, 0)
-        w1_c, w1_s = quantize_weight("w1", w1_bf, [512])
+        w1_bf = cast_weight("w1", w1_raw)
+        b_t, c_t = [], []
+        for pair in range(2):
+            if pair == 1:
+                w1_c, w1_s = quantize_weight("w1", w1_bf, [512])
+            fetched = keep.tile(
+                [P, PACK, S], BF16, name="fetched%d" % pair, align_bytes=64, tag=("fetched0", "w1_bf")[pair]
+            )
+            for u in range(2):
+                t = 2 * pair + u
+                b_t.append(fetched[:, 2 * u, :])
+                c_t.append(fetched[:, 2 * u + 1, :])
+                nc.vector.tensor_copy(b_t[t], wide[t][:].indirect(n2_l[:]))
+                nc.vector.tensor_copy(c_t[t], wide[t][:].indirect(n3_l[:]))
         y_t, yh_t = [], []
         for t in range(PACK):
             bank = psum.tile([P, S], F32, name="bank_y%d" % t, tag="b%d" % t)
-            product(bank, w1_c, w1_s, t, offs_w, offs_b, every)
+            product(bank[:], w1_c, w1_s, t, offs_w, offs_b, every)
             y = keep.tile([P, S], F32, name="y%d" % t)
             yh = keep.tile([P, S], F32, name="yh%d" % t)
             nc.scalar.activation(yh[:], bank[:], ACT.Copy, scale=neg[:, t : t + 1])
@@ -167,68 +168,88 @@ def tile_picked_twcclampbhopg_none_p_kernel(
             y_t.append(y)
             yh_t.append(yh)
 
-        cand_w = keep.tile([P, S], U32, name="cand_w", align_bytes=64)
-        nc.vector.tensor_copy(
-            cand_w[:].rearrange("p (t m) -> p m t", t=PACK), xw[:].indirect(cand_l[:])
-        )
-        for t in range(PACK):
-            fetch_d(t, 1)
+        z_bf = keep.tile([P, S, PACK], BF16, name="z_bf", align_bytes=64)
+        pieces = [(0, every), (1, every)] + [(t, c) for c in halves for t in (2, 3)]
+        last = len(pieces) - 1
+        a_t, lo_t = {}, {}
+        for step in range(len(pieces) + 2):
+            if step <= last:
+                t, c = pieces[step]
+                width = c.stop - c.start
+                a_t[step] = keep.tile(
+                    [P, width], F32, name="a%d" % step, align_bytes=64, tag="late" if step == last else "am%d" % step
+                )
+                for c0 in range(c.start, c.stop, HALF):
+                    nc.vector.tensor_tensor(
+                        a_t[step][:, c0 - c.start : c0 - c.start + HALF],
+                        yh_t[t][:].indirect(entries(n1_l, slice(c0, c0 + HALF))),
+                        y_t[t][:, c0 : c0 + HALF],
+                        ALU.add,
+                    )
+            if step >= 2:
+                i = step - 2
+                t, c = pieces[i]
+                hi = keep.tile([P, c.stop - c.start], BF16, name="hi%d" % i)
+                nc.vector.tensor_tensor(hi[:], lo_t[i][:], c_t[t][:, c], ALU.max)
+                nc.scalar.activation(z_bf[:, c, t], hi[:], ACT.Copy, scale=sgn[:, t : t + 1])
+            if 1 <= step <= last + 1:
+                i = step - 1
+                t, c = pieces[i]
+                lo_t[i] = keep.tile([P, c.stop - c.start], BF16, name="lo%d" % i)
+                nc.vector.tensor_tensor(lo_t[i][:], a_t[i][:], b_t[t][:, c], ALU.min)
 
+        cand_w = keep.tile([P, S], U32, name="cand_w", align_bytes=64, tag="late")
+        nc.vector.tensor_copy(
+            cand_w[:].rearrange("p (t g r) -> p g t r", t=PACK, g=8), xw[:].indirect(cand_l[:])
+        )
         z_c = keep.tile([P, S], U32, name="z_c", align_bytes=64)
         z_s = keep.tile([P, S], U8, name="z_s", align_bytes=64)
-        s_bank = [psum.tile([P, S], F32, name="bank_s%d" % t, tag="a%d" % t) for t in range(PACK)]
-        s_t = [keep.tile([P, S], F32, name="s%d" % t) for t in range(PACK)]
-        for h in range(2):
-            z_bf = keep.tile([P, HALF, PACK], BF16, name="z_bf%d" % h, align_bytes=64)
-            a_t = [keep.tile([P, HALF], F32, name="a%d_%d" % (t, h)) for t in range(PACK)]
-            lo_t = [keep.tile([P, HALF], BF16, name="lo%d_%d" % (t, h)) for t in range(PACK)]
-            hi_t = [keep.tile([P, HALF], BF16, name="hi%d_%d" % (t, h)) for t in range(PACK)]
-            for step in range(PACK + 2):
-                if step < PACK:
-                    t = step
-                    nc.vector.tensor_tensor(
-                        a_t[t][:], yh_t[t][:].indirect(part(n1_l, h)), y_t[t][:, cols(h)], ALU.add
-                    )
-                if 1 <= step <= PACK:
-                    t = step - 1
-                    nc.vector.tensor_tensor(lo_t[t][:], a_t[t][:], b_t[t][:, cols(h)], ALU.min)
-                if step >= 2:
-                    t = step - 2
-                    nc.vector.tensor_tensor(hi_t[t][:], lo_t[t][:], c_t[t][:, cols(h)], ALU.max)
-                    nc.scalar.activation(z_bf[:, :, t], hi_t[t][:], ACT.Copy, scale=sgn[:, t : t + 1])
+        for c in halves:
             nc.vector.quantize_mx(
-                out=z_c[:, cols(h)].bitcast(FP8X4),
-                scales=z_s[:, cols(h)],
-                in_=z_bf[:].rearrange("p c t -> p (c t)"),
+                out=z_c[:, c].bitcast(FP8X4),
+                scales=z_s[:, c],
+                in_=z_bf[:, c, :].rearrange("p c t -> p (c t)"),
             )
+        s_bank = {}
+        for h, c in enumerate(halves):
             for t in range(PACK):
-                product(s_bank[t], cand_w, cand_b, t, z_c, z_s, cols(h))
-                if h == 0 or t == 0:
-                    nc.scalar.activation(s_t[t][:, cols(h)], s_bank[t][:, cols(h)], ACT.Copy, scale=0.0625)
+                s_bank[t, h] = psum.tile([P, HALF], F32, name="bank_s%d_%d" % (t, h), tag="%s%d" % ("ab"[h], t))
+                product(s_bank[t, h][:], cand_w, cand_b, t, z_c, z_s, c)
+                if t == 0:
+                    nc.scalar.activation(wide[t][:, c], s_bank[t, h][:], ACT.Copy, scale=0.0625)
                 else:
-                    nc.vector.tensor_scalar_mul(s_t[t][:, cols(h)], s_bank[t][:, cols(h)], 0.0625)
+                    nc.vector.tensor_scalar_mul(wide[t][:, c], s_bank[t, h][:], 0.0625)
 
-        out_rows = out.rearrange("(p t) j -> t p j", t=PACK)
-        sig_t = [keep.tile([P, S], F32, name="sig%d" % t) for t in range(PACK)]
-        st_t = [keep.tile([P, S], F32, name="st%d" % t) for t in range(PACK)]
+        out_rows = out.rearrange("(g t r) j -> t g r j", t=PACK, g=8)
+        sig_t = [keep.tile([P, S], F32, name="sig%d" % t, tag="sig%d" % t) for t in range(PACK)]
         for t in range(PACK):
-            for h in range(2):
-                nc.scalar.activation(sig_t[t][:, cols(h)], s_t[t][:].indirect(part(n4_l, h)), ACT.Sigmoid)
-            nc.vector.tensor_tensor(st_t[t][:], s_t[t][:], sig_t[t][:], ALU.mult)
-        for t in range(PACK):
-            if t in [0]:
-                for h in range(2):
-                    far = keep.tile([P, HALF], F32, name="far%d_%d" % (t, h))
-                    nc.vector.tensor_copy(far[:], st_t[t][:].indirect(part(n5_l, h)))
-                    res = keep.tile([P, HALF], F32, name="res%d_%d" % (t, h))
-                    nc.vector.tensor_tensor(res[:], st_t[t][:, cols(h)], far[:], ALU.subtract)
-                    nc.sync.dma_start(out_rows[t][:, cols(h)], res[:])
-            else:
-                minus = keep.tile([P, S], F32, name="minus%d" % t)
-                nc.scalar.activation(minus[:], st_t[t][:], ACT.Copy, scale=-1.0)
-                for h in range(2):
-                    res = keep.tile([P, HALF], F32, name="res%d_%d" % (t, h))
-                    nc.vector.tensor_tensor(
-                        res[:], minus[:].indirect(part(n5_l, h)), st_t[t][:, cols(h)], ALU.add
-                    )
-                    nc.sync.dma_start(out_rows[t][:, cols(h)], res[:])
+            for c in (halves if t == 0 else [every]):
+                nc.scalar.activation(sig_t[t][:, c], wide[t][:].indirect(entries(n4_l, c)), ACT.Sigmoid)
+
+        def gate(t, slot, minus):
+            st = keep.tile([P, S], F32, name="st%d" % t, tag=slot)
+            for h, c in enumerate(halves):
+                nc.vector.scalar_tensor_tensor(
+                    st[:, c], s_bank[t, h][:], 0.0625, sig_t[t][:, c], ALU.mult, ALU.mult
+                )
+                if t == 0:
+                    nc.vector.tensor_scalar_mul(minus[:, c], st[:, c], -1.0)
+            if t > 0:
+                nc.scalar.activation(minus[:, every], st[:], ACT.Copy, scale=-1.0)
+            return st
+
+        def finish(t, st, minus, steps, stores):
+            res = keep.tile([P, S], F32, name="res%d" % t)
+            for c in steps:
+                nc.vector.tensor_tensor(res[:, c], minus[:].indirect(entries(n5_l, c)), st[:, c], ALU.add)
+            for c in stores:
+                nc.sync.dma_start(out_rows[t][:, :, c], res[:, c])
+
+        minus0 = keep.tile([P, S], F32, name="minus0", tag="minus0")
+        finish(0, gate(0, "st0", minus0), minus0, halves, [every])
+        windows = {1: wide[0], 2: wide[1], 3: keep.tile([P, S], F32, name="minus3")}
+        st_t = {t: gate(t, slot, windows[t]) for t, slot in ((1, "st0"), (2, "minus0"), (3, "sig2"))}
+        tail = [slice(0, 256), slice(256, 384), slice(384, 512)]
+        for t in range(1, PACK):
+            steps = tail if t == PACK - 1 else [every]
+            finish(t, st_t[t], windows[t], steps, steps)

@@ -140,8 +140,8 @@ def tile_picked_twcclampbhopg_none_p_kernel(
 
         cand_b = keep.tile([P, S], U8, name="cand_b", align_bytes=64)
         nc.vector.tensor_copy(
-            cand_b[:].bitcast(I32).rearrange("p (t g r) -> p t g r", t=PACK, g=8),
-            cand_b0[:].bitcast(I32).rearrange("p (g t r) -> p t g r", t=PACK, g=8),
+            cand_b[:].bitcast(I32).rearrange("p (t g r) -> p t g r", t=PACK, g=16),
+            cand_b0[:].bitcast(I32).rearrange("p (g t r) -> p t g r", t=PACK, g=16),
         )
         w1_bf = cast_weight("w1", w1_raw)
         b_t, c_t = [], []
@@ -200,7 +200,7 @@ def tile_picked_twcclampbhopg_none_p_kernel(
 
         cand_w = keep.tile([P, S], U32, name="cand_w", align_bytes=64, tag="late")
         nc.vector.tensor_copy(
-            cand_w[:].rearrange("p (t g r) -> p g t r", t=PACK, g=8), xw[:].indirect(cand_l[:])
+            cand_w[:].rearrange("p (t g r) -> p g t r", t=PACK, g=16), xw[:].indirect(cand_l[:])
         )
         z_c = keep.tile([P, S], U32, name="z_c", align_bytes=64)
         z_s = keep.tile([P, S], U8, name="z_s", align_bytes=64)
@@ -220,7 +220,7 @@ def tile_picked_twcclampbhopg_none_p_kernel(
                 else:
                     nc.vector.tensor_scalar_mul(wide[t][:, c], s_bank[t, h][:], 0.0625)
 
-        out_rows = out.rearrange("(g t r) j -> t g r j", t=PACK, g=8)
+        out_rows = out.rearrange("(g t r) j -> t g r j", t=PACK, g=16)
         sig_t = [keep.tile([P, S], F32, name="sig%d" % t, tag="sig%d" % t) for t in range(PACK)]
         for t in range(PACK):
             for c in (halves if t == 0 else [every]):
@@ -247,9 +247,9 @@ def tile_picked_twcclampbhopg_none_p_kernel(
 
         minus0 = keep.tile([P, S], F32, name="minus0", tag="minus0")
         finish(0, gate(0, "st0", minus0), minus0, halves, [every])
-        windows = {1: wide[0], 2: wide[1], 3: keep.tile([P, S], F32, name="minus3")}
+        windows = {1: wide[0], 2: wide[1], 3: wide[2]}
         st_t = {t: gate(t, slot, windows[t]) for t, slot in ((1, "st0"), (2, "minus0"), (3, "sig2"))}
-        tail = [slice(0, 256), slice(256, 384), slice(384, 512)]
+        tail = halves
         for t in range(1, PACK):
             steps = tail if t == PACK - 1 else [every]
             finish(t, st_t[t], windows[t], steps, steps)

@@ -5,9 +5,11 @@ import concourse.mybir as mybir
 K, T, S = 512, 2048, 512
 P = 128
 PACK = 4
-HALF = 256
-FIRST = 256
-FLOPS = 3 * 2 * 512 * 512 * 512
+HALF = S // 2
+PER_COLUMN = 16
+GROUPS = 16
+SCORE_SCALE = 0.0625
+FLOPS = 3 * 2 * K * S * S
 
 F32 = mybir.dt.float32
 BF16 = mybir.dt.bfloat16
@@ -33,7 +35,7 @@ def tile_picked_twcclampbhopg_none_p_kernel(
         halves = [slice(0, HALF), slice(HALF, S)]
 
         def load_list(name, src):
-            tile = lists.tile([P, S // 16], U16, name=name)
+            tile = lists.tile([P, S // PER_COLUMN], U16, name=name)
             nc.sync.dma_start(tile[:], src)
             return tile
 
@@ -43,7 +45,7 @@ def tile_picked_twcclampbhopg_none_p_kernel(
             return c, raw
 
         def entries(lst, c):
-            return lst[:, c.start // 16 : c.stop // 16]
+            return lst[:, c.start // PER_COLUMN : c.stop // PER_COLUMN]
 
         warm = keep.tile([P, 2], F32, name="warm")
         xs = keep.tile([P, T], U8, name="xs", align_bytes=64)
@@ -54,18 +56,18 @@ def tile_picked_twcclampbhopg_none_p_kernel(
         for t in range(PACK):
             nc.vector.memset(wide[t][:, S:], 0.0)
 
-        w2_raw = [load_columns("w2", w2, slice(0, FIRST))]
+        w2_raw = [load_columns("w2", w2, halves[0])]
         scale_rows = x_scales[0].bitcast(I32)
-        for r in range(4):
-            nc.sync.dma_start(xs[r:P:32, :].bitcast(I32), scale_rows[r:16:4, :])
+        for q in range(4):
+            nc.sync.dma_start(xs[q:P:32, :].bitcast(I32), scale_rows[q:16:4, :])
         two_l = load_list("two_l", two)
         offs_l = load_list("offs_l", offs)
-        w2_raw.append(load_columns("w2", w2, slice(FIRST, K)))
         xw = keep.tile([P, T], U32, name="xw", align_bytes=64)
-        nc.sync.dma_start(xw[:].bitcast(I32), x_words[0].rearrange("p n t -> p (n t)").bitcast(I32))
+        nc.sync.dma_start(xw[:].bitcast(I32), x_words[0].rearrange("p n j -> p (n j)").bitcast(I32))
+        w2_raw.append(load_columns("w2", w2, halves[1]))
         cand_l = load_list("cand_l", cand)
-        g_t = keep.tile([P, PACK], F32, name="g_t")
-        nc.sync.dma_start(g_t[:], gs.rearrange("(p t) o -> p (t o)", t=PACK))
+        gain = keep.tile([P, PACK], F32, name="gain")
+        nc.sync.dma_start(gain[:], gs.rearrange("(p t) o -> p (t o)", t=PACK))
         n2_l = load_list("n2_l", n2)
         n3_l = load_list("n3_l", n3)
         w1_raw = [load_columns("w1", w1, c) for c in halves]
@@ -96,8 +98,8 @@ def tile_picked_twcclampbhopg_none_p_kernel(
                 c0 = c0 + width
             return codes, scales
 
-        def pick_bytes(name, lst):
-            picked = keep.tile([P, S], U8, name=name, align_bytes=64)
+        def pick_bytes(name, lst, tag):
+            picked = keep.tile([P, S], U8, name=name, align_bytes=64, tag=tag)
             nc.vector.tensor_copy(picked[:], xs[:].indirect(lst[:]))
             return picked
 
@@ -106,31 +108,30 @@ def tile_picked_twcclampbhopg_none_p_kernel(
             nc.vector.tensor_copy(picked[:], xw[:].indirect(lst[:]))
             return picked
 
-        def product(result, codes, scales, t, words, sbytes, c):
+        def product(result, fixed_words, fixed_scales, t, moving_words, moving_scales, c):
             m = slice(t * P, (t + 1) * P)
             nc.tensor.matmul_mx(
                 out=result,
-                lhsT=codes[:, m].bitcast(FP8X4),
-                lhsT_scale=scales[:, m],
-                rhs=words[:, c].bitcast(FP8X4),
-                rhs_scale=sbytes[:, c],
+                lhsT=fixed_words[:, m].bitcast(FP8X4),
+                lhsT_scale=fixed_scales[:, m],
+                rhs=moving_words[:, c].bitcast(FP8X4),
+                rhs_scale=moving_scales[:, c],
                 start=True,
                 stop=True,
             )
 
         w2_bf = cast_weight("w2", w2_raw)
-        two_b = pick_bytes("two_b", two_l)
-        offs_b = pick_bytes("offs_b", offs_l)
-        cand_b0 = pick_bytes("cand_b0", cand_l)
-        w2_c, w2_s = quantize_weight("w2", w2_bf, [128, 128, 256])
+        two_b = pick_bytes("two_b", two_l, "two_b")
+        offs_b = pick_bytes("offs_b", offs_l, "offs_b")
         two_w = pick_words("two_w", two_l)
+        w2_c, w2_s = quantize_weight("w2", w2_bf, [P, P, 2 * P])
 
         mag = keep.tile([P, PACK], F32, name="mag")
-        sgn = keep.tile([P, PACK], F32, name="sgn")
-        neg = keep.tile([P, PACK], F32, name="neg")
-        nc.scalar.activation(mag[:], g_t[:], ACT.Abs)
-        nc.scalar.activation(neg[:], mag[:], ACT.Copy, scale=-0.5)
-        nc.scalar.activation(sgn[:], g_t[:], ACT.Sign)
+        sign = keep.tile([P, PACK], F32, name="sign")
+        less_half = keep.tile([P, PACK], F32, name="less_half")
+        nc.scalar.activation(mag[:], gain[:], ACT.Abs)
+        nc.scalar.activation(less_half[:], mag[:], ACT.Copy, scale=-0.5)
+        nc.scalar.activation(sign[:], gain[:], ACT.Sign)
 
         offs_w = pick_words("offs_w", offs_l)
         for t in range(PACK):
@@ -138,69 +139,76 @@ def tile_picked_twcclampbhopg_none_p_kernel(
             product(bank[:], w2_c, w2_s, t, two_w, two_b, every)
             nc.scalar.activation(wide[t][:, every], bank[:], ACT.Copy, scale=mag[:, t : t + 1])
 
+        cand_listed_b = pick_bytes("cand_listed_b", cand_l, "w2_bf")
         cand_b = keep.tile([P, S], U8, name="cand_b", align_bytes=64)
         nc.vector.tensor_copy(
-            cand_b[:].bitcast(I32).rearrange("p (t g r) -> p t g r", t=PACK, g=16),
-            cand_b0[:].bitcast(I32).rearrange("p (g t r) -> p t g r", t=PACK, g=16),
+            cand_b[:].bitcast(I32).rearrange("p (t u r) -> p t u r", t=PACK, u=GROUPS),
+            cand_listed_b[:].bitcast(I32).rearrange("p (u t r) -> p t u r", t=PACK, u=GROUPS),
         )
+
         w1_bf = cast_weight("w1", w1_raw)
         b_t, c_t = [], []
-        for pair in range(2):
-            if pair == 1:
-                w1_c, w1_s = quantize_weight("w1", w1_bf, [512])
-            fetched = keep.tile(
-                [P, PACK, S], BF16, name="fetched%d" % pair, align_bytes=64, tag=("fetched0", "w1_bf")[pair]
-            )
-            for u in range(2):
-                t = 2 * pair + u
-                b_t.append(fetched[:, 2 * u, :])
-                c_t.append(fetched[:, 2 * u + 1, :])
+
+        def fetch_d(pair, tag):
+            fetched = keep.tile([P, PACK, S], BF16, name="fetched%d" % pair, align_bytes=64, tag=tag)
+            for member in range(2):
+                t = 2 * pair + member
+                b_t.append(fetched[:, 2 * member, :])
+                c_t.append(fetched[:, 2 * member + 1, :])
                 nc.vector.tensor_copy(b_t[t], wide[t][:].indirect(n2_l[:]))
                 nc.vector.tensor_copy(c_t[t], wide[t][:].indirect(n3_l[:]))
-        y_t, yh_t = [], []
+
+        fetch_d(0, "fetched0")
+        w1_c, w1_s = quantize_weight("w1", w1_bf, [K])
+        fetch_d(1, "w1_bf")
+
+        y_t, less_half_y_t = [], []
         for t in range(PACK):
             bank = psum.tile([P, S], F32, name="bank_y%d" % t, tag="b%d" % t)
             product(bank[:], w1_c, w1_s, t, offs_w, offs_b, every)
             y = keep.tile([P, S], F32, name="y%d" % t)
-            yh = keep.tile([P, S], F32, name="yh%d" % t)
-            nc.scalar.activation(yh[:], bank[:], ACT.Copy, scale=neg[:, t : t + 1])
+            less_half_y = keep.tile([P, S], F32, name="less_half_y%d" % t)
+            nc.scalar.activation(less_half_y[:], bank[:], ACT.Copy, scale=less_half[:, t : t + 1])
             nc.scalar.activation(y[:], bank[:], ACT.Copy, scale=mag[:, t : t + 1])
             y_t.append(y)
-            yh_t.append(yh)
+            less_half_y_t.append(less_half_y)
 
         z_bf = keep.tile([P, S, PACK], BF16, name="z_bf", align_bytes=64)
         pieces = [(0, every), (1, every)] + [(t, c) for c in halves for t in (2, 3)]
         last = len(pieces) - 1
-        a_t, lo_t = {}, {}
+        a_t, low_t = {}, {}
         for step in range(len(pieces) + 2):
             if step <= last:
                 t, c = pieces[step]
-                width = c.stop - c.start
                 a_t[step] = keep.tile(
-                    [P, width], F32, name="a%d" % step, align_bytes=64, tag="late" if step == last else "am%d" % step
+                    [P, c.stop - c.start],
+                    F32,
+                    name="a%d" % step,
+                    align_bytes=64,
+                    tag="a_last" if step == last else "a_piece%d" % step,
                 )
                 for c0 in range(c.start, c.stop, HALF):
                     nc.vector.tensor_tensor(
                         a_t[step][:, c0 - c.start : c0 - c.start + HALF],
-                        yh_t[t][:].indirect(entries(n1_l, slice(c0, c0 + HALF))),
+                        less_half_y_t[t][:].indirect(entries(n1_l, slice(c0, c0 + HALF))),
                         y_t[t][:, c0 : c0 + HALF],
                         ALU.add,
                     )
             if step >= 2:
                 i = step - 2
                 t, c = pieces[i]
-                hi = keep.tile([P, c.stop - c.start], BF16, name="hi%d" % i)
-                nc.vector.tensor_tensor(hi[:], lo_t[i][:], c_t[t][:, c], ALU.max)
-                nc.scalar.activation(z_bf[:, c, t], hi[:], ACT.Copy, scale=sgn[:, t : t + 1])
+                high = keep.tile([P, c.stop - c.start], BF16, name="high%d" % i)
+                nc.vector.tensor_tensor(high[:], low_t[i][:], c_t[t][:, c], ALU.max)
+                nc.scalar.activation(z_bf[:, c, t], high[:], ACT.Copy, scale=sign[:, t : t + 1])
             if 1 <= step <= last + 1:
                 i = step - 1
                 t, c = pieces[i]
-                lo_t[i] = keep.tile([P, c.stop - c.start], BF16, name="lo%d" % i)
-                nc.vector.tensor_tensor(lo_t[i][:], a_t[i][:], b_t[t][:, c], ALU.min)
+                low_t[i] = keep.tile([P, c.stop - c.start], BF16, name="low%d" % i)
+                nc.vector.tensor_tensor(low_t[i][:], a_t[i][:], b_t[t][:, c], ALU.min)
 
-        cand_w = keep.tile([P, S], U32, name="cand_w", align_bytes=64, tag="late")
+        cand_w = keep.tile([P, S], U32, name="cand_w", align_bytes=64, tag="a_last")
         nc.vector.tensor_copy(
-            cand_w[:].rearrange("p (t g r) -> p g t r", t=PACK, g=16), xw[:].indirect(cand_l[:])
+            cand_w[:].rearrange("p (t u r) -> p u t r", t=PACK, u=GROUPS), xw[:].indirect(cand_l[:])
         )
         z_c = keep.tile([P, S], U32, name="z_c", align_bytes=64)
         z_s = keep.tile([P, S], U8, name="z_s", align_bytes=64)
@@ -210,46 +218,45 @@ def tile_picked_twcclampbhopg_none_p_kernel(
                 scales=z_s[:, c],
                 in_=z_bf[:, c, :].rearrange("p c t -> p (c t)"),
             )
+
         s_bank = {}
         for h, c in enumerate(halves):
             for t in range(PACK):
                 s_bank[t, h] = psum.tile([P, HALF], F32, name="bank_s%d_%d" % (t, h), tag="%s%d" % ("ab"[h], t))
                 product(s_bank[t, h][:], cand_w, cand_b, t, z_c, z_s, c)
                 if t == 0:
-                    nc.scalar.activation(wide[t][:, c], s_bank[t, h][:], ACT.Copy, scale=0.0625)
+                    nc.scalar.activation(wide[t][:, c], s_bank[t, h][:], ACT.Copy, scale=SCORE_SCALE)
                 else:
-                    nc.vector.tensor_scalar_mul(wide[t][:, c], s_bank[t, h][:], 0.0625)
+                    nc.vector.tensor_scalar_mul(wide[t][:, c], s_bank[t, h][:], SCORE_SCALE)
 
-        out_rows = out.rearrange("(g t r) j -> t g r j", t=PACK, g=16)
         sig_t = [keep.tile([P, S], F32, name="sig%d" % t, tag="sig%d" % t) for t in range(PACK)]
         for t in range(PACK):
-            for c in (halves if t == 0 else [every]):
+            for c in halves if t == 0 else [every]:
                 nc.scalar.activation(sig_t[t][:, c], wide[t][:].indirect(entries(n4_l, c)), ACT.Sigmoid)
 
-        def gate(t, slot, minus):
-            st = keep.tile([P, S], F32, name="st%d" % t, tag=slot)
-            for h, c in enumerate(halves):
-                nc.vector.scalar_tensor_tensor(
-                    st[:, c], s_bank[t, h][:], 0.0625, sig_t[t][:, c], ALU.mult, ALU.mult
-                )
-                if t == 0:
-                    nc.vector.tensor_scalar_mul(minus[:, c], st[:, c], -1.0)
-            if t > 0:
-                nc.scalar.activation(minus[:, every], st[:], ACT.Copy, scale=-1.0)
-            return st
+        out_rows = out.rearrange("(u t r) j -> t u r j", t=PACK, u=GROUPS)
 
-        def finish(t, st, minus, steps, stores):
-            res = keep.tile([P, S], F32, name="res%d" % t)
+        def finish(t, st, minus_st, steps, stores):
+            result = keep.tile([P, S], F32, name="result%d" % t)
             for c in steps:
-                nc.vector.tensor_tensor(res[:, c], minus[:].indirect(entries(n5_l, c)), st[:, c], ALU.add)
+                nc.vector.tensor_tensor(result[:, c], minus_st[:].indirect(entries(n5_l, c)), st[:, c], ALU.add)
             for c in stores:
-                nc.sync.dma_start(out_rows[t][:, :, c], res[:, c])
+                nc.sync.dma_start(out_rows[t][:, :, c], result[:, c])
 
-        minus0 = keep.tile([P, S], F32, name="minus0", tag="minus0")
-        finish(0, gate(0, "st0", minus0), minus0, halves, [every])
-        windows = {1: wide[0], 2: wide[1], 3: wide[2]}
-        st_t = {t: gate(t, slot, windows[t]) for t, slot in ((1, "st0"), (2, "minus0"), (3, "sig2"))}
-        tail = halves
+        minus_st0 = keep.tile([P, S], F32, name="minus_st0", tag="minus_st0")
+        st0 = keep.tile([P, S], F32, name="st0", tag="st0")
+        for h, c in enumerate(halves):
+            for target, factor in ((minus_st0, -SCORE_SCALE), (st0, SCORE_SCALE)):
+                nc.vector.scalar_tensor_tensor(
+                    target[:, c], s_bank[0, h][:], factor, sig_t[0][:, c], ALU.mult, ALU.mult
+                )
+        finish(0, st0, minus_st0, halves, [every])
+
+        st_t = {}
+        for t, tag in ((1, "st0"), (2, "minus_st0"), (3, "sig2")):
+            st_t[t] = keep.tile([P, S], F32, name="st%d" % t, tag=tag)
+            nc.vector.tensor_tensor(st_t[t][:], wide[t][:, every], sig_t[t][:], ALU.mult)
+            nc.scalar.activation(wide[t - 1][:, every], st_t[t][:], ACT.Copy, scale=-1.0)
         for t in range(1, PACK):
-            steps = tail if t == PACK - 1 else [every]
-            finish(t, st_t[t], windows[t], steps, steps)
+            steps = halves if t == PACK - 1 else [every]
+            finish(t, st_t[t], wide[t - 1], steps, steps)

from contextlib import ExitStack

import concourse.mybir as mybir

K, T, S = 512, 2048, 512
P = 128
PACK = 4
HALF = S // 2
PER_COLUMN = 16
GROUPS = 16
SCORE_SCALE = 0.0625
FLOPS = 3 * 2 * K * S * S

F32 = mybir.dt.float32
BF16 = mybir.dt.bfloat16
I32 = mybir.dt.int32
U32 = mybir.dt.uint32
U16 = mybir.dt.uint16
U8 = mybir.dt.uint8
FP8X4 = mybir.dt.float8_e4m3fn_x4
ALU = mybir.AluOpType
ACT = mybir.ActivationFunctionType


def tile_picked_twcclampbhopg_none_p_kernel(
    tc, x_words, x_scales, w1, w2, gs, offs, two, n1, n2, n3, cand, n4, n5, out
):
    nc = tc.nc
    with ExitStack() as ctx:
        lists = ctx.enter_context(tc.tile_pool(name="lists", bufs=1))
        keep = ctx.enter_context(tc.tile_pool(name="keep", bufs=1))
        psum = ctx.enter_context(tc.psum_pool(name="psum", bufs=1))

        every = slice(0, S)
        halves = [slice(0, HALF), slice(HALF, S)]

        def load_list(name, src):
            tile = lists.tile([P, S // PER_COLUMN], U16, name=name)
            nc.sync.dma_start(tile[:], src)
            return tile

        def load_columns(name, w, c):
            raw = keep.tile([P, PACK, c.stop - c.start], F32, name="%s_raw%d" % (name, c.start))
            nc.sync.dma_start(raw[:], w.rearrange("(p j) c -> p j c", j=PACK)[:, :, c])
            return c, raw

        def entries(lst, c):
            return lst[:, c.start // PER_COLUMN : c.stop // PER_COLUMN]

        warm = keep.tile([P, 2], F32, name="warm")
        xs = keep.tile([P, T], U8, name="xs", align_bytes=64)
        nc.vector.memset(xs[:].bitcast(I32), 0)
        nc.vector.memset(warm[:, 0:1], 0.0)
        nc.scalar.activation(warm[:, 1:2], warm[:, 0:1], ACT.Sigmoid)
        wide = [keep.tile([P, 2 * S], F32, name="wide%d" % t) for t in range(PACK)]
        for t in range(PACK):
            nc.vector.memset(wide[t][:, S:], 0.0)

        w2_raw = [load_columns("w2", w2, halves[0])]
        scale_rows = x_scales[0].bitcast(I32)
        for q in range(4):
            nc.sync.dma_start(xs[q:P:32, :].bitcast(I32), scale_rows[q:16:4, :])
        two_l = load_list("two_l", two)
        offs_l = load_list("offs_l", offs)
        xw = keep.tile([P, T], U32, name="xw", align_bytes=64)
        nc.sync.dma_start(xw[:].bitcast(I32), x_words[0].rearrange("p n j -> p (n j)").bitcast(I32))
        w2_raw.append(load_columns("w2", w2, halves[1]))
        cand_l = load_list("cand_l", cand)
        gain = keep.tile([P, PACK], F32, name="gain")
        nc.sync.dma_start(gain[:], gs.rearrange("(p t) o -> p (t o)", t=PACK))
        n2_l = load_list("n2_l", n2)
        n3_l = load_list("n3_l", n3)
        w1_raw = [load_columns("w1", w1, c) for c in halves]
        n1_l = load_list("n1_l", n1)
        n4_l = load_list("n4_l", n4)
        n5_l = load_list("n5_l", n5)

        def cast_weight(name, parts):
            grouped = keep.tile([P, PACK * K], BF16, name=name + "_bf", align_bytes=64, tag=name + "_bf")
            view = grouped[:].rearrange("p (t m j) -> p m j t", t=PACK, j=PACK)
            for c, raw in parts:
                nc.scalar.copy(
                    view[:, c.start // PACK : c.stop // PACK],
                    raw[:].rearrange("p j (m t) -> p m j t", t=PACK),
                )
            return grouped

        def quantize_weight(name, grouped, widths):
            codes = keep.tile([P, K], U32, name=name + "_codes", align_bytes=64)
            scales = keep.tile([P, K], U8, name=name + "_scales", align_bytes=64)
            c0 = 0
            for width in widths:
                nc.vector.quantize_mx(
                    out=codes[:, c0 : c0 + width].bitcast(FP8X4),
                    scales=scales[:, c0 : c0 + width],
                    in_=grouped[:, PACK * c0 : PACK * (c0 + width)],
                )
                c0 = c0 + width
            return codes, scales

        def pick_bytes(name, lst, tag):
            picked = keep.tile([P, S], U8, name=name, align_bytes=64, tag=tag)
            nc.vector.tensor_copy(picked[:], xs[:].indirect(lst[:]))
            return picked

        def pick_words(name, lst):
            picked = keep.tile([P, S], U32, name=name, align_bytes=64)
            nc.vector.tensor_copy(picked[:], xw[:].indirect(lst[:]))
            return picked

        def product(result, fixed_words, fixed_scales, t, moving_words, moving_scales, c):
            m = slice(t * P, (t + 1) * P)
            nc.tensor.matmul_mx(
                out=result,
                lhsT=fixed_words[:, m].bitcast(FP8X4),
                lhsT_scale=fixed_scales[:, m],
                rhs=moving_words[:, c].bitcast(FP8X4),
                rhs_scale=moving_scales[:, c],
                start=True,
                stop=True,
            )

        w2_bf = cast_weight("w2", w2_raw)
        two_b = pick_bytes("two_b", two_l, "two_b")
        offs_b = pick_bytes("offs_b", offs_l, "offs_b")
        two_w = pick_words("two_w", two_l)
        w2_c, w2_s = quantize_weight("w2", w2_bf, [P, P, 2 * P])

        mag = keep.tile([P, PACK], F32, name="mag")
        sign = keep.tile([P, PACK], F32, name="sign")
        less_half = keep.tile([P, PACK], F32, name="less_half")
        nc.scalar.activation(mag[:], gain[:], ACT.Abs)
        nc.scalar.activation(less_half[:], mag[:], ACT.Copy, scale=-0.5)
        nc.scalar.activation(sign[:], gain[:], ACT.Sign)

        offs_w = pick_words("offs_w", offs_l)
        for t in range(PACK):
            bank = psum.tile([P, S], F32, name="bank_d%d" % t, tag="a%d" % t)
            product(bank[:], w2_c, w2_s, t, two_w, two_b, every)
            nc.scalar.activation(wide[t][:, every], bank[:], ACT.Copy, scale=mag[:, t : t + 1])

        cand_listed_b = pick_bytes("cand_listed_b", cand_l, "w2_bf")
        cand_b = keep.tile([P, S], U8, name="cand_b", align_bytes=64)
        nc.vector.tensor_copy(
            cand_b[:].bitcast(I32).rearrange("p (t u r) -> p t u r", t=PACK, u=GROUPS),
            cand_listed_b[:].bitcast(I32).rearrange("p (u t r) -> p t u r", t=PACK, u=GROUPS),
        )

        w1_bf = cast_weight("w1", w1_raw)
        b_t, c_t = [], []

        def fetch_d(pair, tag):
            fetched = keep.tile([P, PACK, S], BF16, name="fetched%d" % pair, align_bytes=64, tag=tag)
            for member in range(2):
                t = 2 * pair + member
                b_t.append(fetched[:, 2 * member, :])
                c_t.append(fetched[:, 2 * member + 1, :])
                nc.vector.tensor_copy(b_t[t], wide[t][:].indirect(n2_l[:]))
                nc.vector.tensor_copy(c_t[t], wide[t][:].indirect(n3_l[:]))

        fetch_d(0, "fetched0")
        w1_c, w1_s = quantize_weight("w1", w1_bf, [K])
        fetch_d(1, "w1_bf")

        y_t, less_half_y_t = [], []
        for t in range(PACK):
            bank = psum.tile([P, S], F32, name="bank_y%d" % t, tag="b%d" % t)
            product(bank[:], w1_c, w1_s, t, offs_w, offs_b, every)
            y = keep.tile([P, S], F32, name="y%d" % t)
            less_half_y = keep.tile([P, S], F32, name="less_half_y%d" % t)
            nc.scalar.activation(less_half_y[:], bank[:], ACT.Copy, scale=less_half[:, t : t + 1])
            nc.scalar.activation(y[:], bank[:], ACT.Copy, scale=mag[:, t : t + 1])
            y_t.append(y)
            less_half_y_t.append(less_half_y)

        z_bf = keep.tile([P, S, PACK], BF16, name="z_bf", align_bytes=64)
        pieces = [(0, every), (1, every)] + [(t, c) for c in halves for t in (2, 3)]
        last = len(pieces) - 1
        a_t, low_t = {}, {}
        for step in range(len(pieces) + 2):
            if step <= last:
                t, c = pieces[step]
                a_t[step] = keep.tile(
                    [P, c.stop - c.start],
                    F32,
                    name="a%d" % step,
                    align_bytes=64,
                    tag="a_last" if step == last else "a_piece%d" % step,
                )
                for c0 in range(c.start, c.stop, HALF):
                    nc.vector.tensor_tensor(
                        a_t[step][:, c0 - c.start : c0 - c.start + HALF],
                        less_half_y_t[t][:].indirect(entries(n1_l, slice(c0, c0 + HALF))),
                        y_t[t][:, c0 : c0 + HALF],
                        ALU.add,
                    )
            if step >= 2:
                i = step - 2
                t, c = pieces[i]
                high = keep.tile([P, c.stop - c.start], BF16, name="high%d" % i)
                nc.vector.tensor_tensor(high[:], low_t[i][:], c_t[t][:, c], ALU.max)
                nc.scalar.activation(z_bf[:, c, t], high[:], ACT.Copy, scale=sign[:, t : t + 1])
            if 1 <= step <= last + 1:
                i = step - 1
                t, c = pieces[i]
                low_t[i] = keep.tile([P, c.stop - c.start], BF16, name="low%d" % i)
                nc.vector.tensor_tensor(low_t[i][:], a_t[i][:], b_t[t][:, c], ALU.min)

        cand_w = keep.tile([P, S], U32, name="cand_w", align_bytes=64, tag="a_last")
        nc.vector.tensor_copy(
            cand_w[:].rearrange("p (t u r) -> p u t r", t=PACK, u=GROUPS), xw[:].indirect(cand_l[:])
        )
        z_c = keep.tile([P, S], U32, name="z_c", align_bytes=64)
        z_s = keep.tile([P, S], U8, name="z_s", align_bytes=64)
        for c in halves:
            nc.vector.quantize_mx(
                out=z_c[:, c].bitcast(FP8X4),
                scales=z_s[:, c],
                in_=z_bf[:, c, :].rearrange("p c t -> p (c t)"),
            )

        s_bank = {}
        for h, c in enumerate(halves):
            for t in range(PACK):
                s_bank[t, h] = psum.tile([P, HALF], F32, name="bank_s%d_%d" % (t, h), tag="%s%d" % ("ab"[h], t))
                product(s_bank[t, h][:], cand_w, cand_b, t, z_c, z_s, c)
                if t == 0:
                    nc.scalar.activation(wide[t][:, c], s_bank[t, h][:], ACT.Copy, scale=SCORE_SCALE)
                else:
                    nc.vector.tensor_scalar_mul(wide[t][:, c], s_bank[t, h][:], SCORE_SCALE)

        sig_t = [keep.tile([P, S], F32, name="sig%d" % t, tag="sig%d" % t) for t in range(PACK)]
        for t in range(PACK):
            for c in halves if t == 0 else [every]:
                nc.scalar.activation(sig_t[t][:, c], wide[t][:].indirect(entries(n4_l, c)), ACT.Sigmoid)

        out_rows = out.rearrange("(u t r) j -> t u r j", t=PACK, u=GROUPS)

        def finish(t, st, minus_st, steps, stores):
            result = keep.tile([P, S], F32, name="result%d" % t)
            for c in steps:
                nc.vector.tensor_tensor(result[:, c], minus_st[:].indirect(entries(n5_l, c)), st[:, c], ALU.add)
            for c in stores:
                nc.sync.dma_start(out_rows[t][:, :, c], result[:, c])

        minus_st0 = keep.tile([P, S], F32, name="minus_st0", tag="minus_st0")
        st0 = keep.tile([P, S], F32, name="st0", tag="st0")
        for h, c in enumerate(halves):
            for target, factor in ((minus_st0, -SCORE_SCALE), (st0, SCORE_SCALE)):
                nc.vector.scalar_tensor_tensor(
                    target[:, c], s_bank[0, h][:], factor, sig_t[0][:, c], ALU.mult, ALU.mult
                )
        finish(0, st0, minus_st0, halves, [every])

        st_t = {}
        for t, tag in ((1, "st0"), (2, "minus_st0"), (3, "sig2")):
            st_t[t] = keep.tile([P, S], F32, name="st%d" % t, tag=tag)
            nc.vector.tensor_tensor(st_t[t][:], wide[t][:, every], sig_t[t][:], ALU.mult)
            nc.scalar.activation(wide[t - 1][:, every], st_t[t][:], ACT.Copy, scale=-1.0)
        for t in range(1, PACK):
            steps = halves if t == PACK - 1 else [every]
            finish(t, st_t[t], wide[t - 1], steps, steps)
